import numpy as np, ml_dtypes
CORES = [40,64,80,88,96,104,120,144]
N = 8
BF = ml_dtypes.bfloat16
def gentries(a):
    return np.ascontiguousarray(a.reshape(8, 16, -1).transpose(0, 2, 1)).reshape(8, -1)
def gtable(e):
    e = np.asarray(e); return np.ascontiguousarray(e.reshape(8, -1, 16).transpose(0, 2, 1)).reshape(128, -1).astype(np.int32)
W, H, L, CAP, RO = 1280, 512, 256, 192, 3
def pick(t, e):
    return np.take_along_axis(t, e[:, None, :], 2)
def at(x, c):
    return pick(x, c.reshape(8, -1)).reshape(8, 16, 16, -1)
def moved(v, dl):
    return np.clip(v + dl[:, :, None, :], 0, 63)
def spot(u):
    return (((u * u) >> 5) + 37 * u) & (H - 1)
def parts(rng):
    x = rng.integers(0, 64, (N, 8, 16, W)); su = rng.integers(0, W, (N, 8, 16, W)); co = np.argsort(rng.random((N, 8, 16, W)), axis=-1)
    dl = rng.integers(-20, 21, (N, 8, 16, L)); la = rng.integers(0, W, (N, 8, L)); lb = rng.integers(0, W, (N, 8, L))
    wt = rng.integers(0, 256, (N, 8, 16)); th = 110 + 20 * np.argsort(rng.random((N, 8)), axis=-1) + rng.integers(0, 20, (N, 8))
    return x, su, co, dl, la, lb, wt, th
def pack(x, su, co, dl, la, lb, wt, th):
    fl = lambda a, n: np.ascontiguousarray(np.asarray(a).reshape(N, 128, n)).astype(np.float32).astype(BF)
    it = lambda a: np.ascontiguousarray(np.asarray(a).reshape(N, 128, W)).astype(np.int32)
    return {"x0": fl(x, W), "su": it(su), "co": it(co), "dl": fl(dl, L), "la": np.stack([gtable(a) for a in la]), "lb": np.stack([gtable(a) for a in lb]),
            "wt": fl(wt, 1), "th": np.asarray(th).reshape(N, 8, 1).astype(np.int32)}
def put(p, c, v):
    w = np.argmax(p == v[..., None], axis=-1); old = p[..., c].copy()
    np.put_along_axis(p, w[..., None], old[..., None], -1); p[..., c] = v
def two(rng, n):
    c = rng.integers(0, 3, (N, 8, 1, n)); return np.where(c < 2, c, rng.integers(0, 2, (N, 8, 16, n)))
def spots(dl, wt):
    return spot(np.sum(63 * wt[:, :, None] * (dl > 0), axis=1) & 4095)
def setup_inputs(rng):
    return pack(*parts(rng))
def setup_inputs_spread(rng):
    x, su, co, dl, la, lb, wt, th = parts(rng)
    p = np.exp2(rng.integers(-2, 3, (N, 8, 1, W))); x = np.minimum((64 * rng.random((N, 8, 16, W)) ** p).astype(np.int64), 63)
    p = np.exp2(rng.integers(-2, 3, (N, 8, 1, W))); su = np.minimum((W * rng.random((N, 8, 16, W)) ** p).astype(np.int64), W - 1)
    dl = np.rint((2 * rng.random((N, 8, 16, L)) - 1) * rng.choice(np.array([0, 1, 3, 9, 27, 63]), (N, 8, 1, L))).astype(np.int64)
    la = np.minimum((W * rng.random((N, 8, L)) ** 2).astype(np.int64), W - 1); lb = W - 1 - np.minimum((W * rng.random((N, 8, L)) ** 2).astype(np.int64), W - 1)
    wt = np.minimum(np.exp2(8 * rng.random((N, 8, 16))).astype(np.int64), 256) - 1
    th = np.where(rng.random((N, 8)) < 0.5, np.minimum(np.exp2(10 * rng.random((N, 8))).astype(np.int64), 1024) - 1, rng.integers(100, 300, (N, 8)))
    return pack(x, su, co, dl, la, lb, wt, th)
def setup_inputs_ends(rng):
    x, su, co, dl, la, lb, wt, th = parts(rng)
    x = 63 * two(rng, W); su = (W - 1) * two(rng, W); dl = 126 * two(rng, L) - 63
    la = (W - 1) * rng.integers(0, 2, (N, 8, L)); lb = (W - 1) * rng.integers(0, 2, (N, 8, L)); la[:, :, L - 1] = W - 1; lb[:, :, 0] = 0
    wt = 255 * rng.integers(0, 2, (N, 8, 16)); wt[:, 0] = 255 * (np.arange(16) & 1); wt[:, 7] = 255
    th = 1023 * rng.integers(0, 2, (N, 8)); th[:, 0] = 1023; th[:, 1] = 0; th[:, 7] = 0; th[0, 6] = 1023
    z = rng.integers(0, 2, (N, 8, 16)); z[:, :, 0] = 1; z[:, :, 15] = 0
    put(co, 0, (W - 1) * z); put(co, W - 1, (W - 1) * (1 - z))
    dl[:, 7] = np.where(rng.random((N, 1, L)) < 0.5, 63, -63); dl[:, 7, :, 0] = 63; dl[:, 7, :, 1] = -63; dl[:, 7, :, L - 1] = 63
    x[:, 7, :, 0] = 0; x[:, 7, :, W - 1] = 0; x[:, 7, :, spot((16 * 63 * 255) & 4095)] = 0
    x[:, 6, :, 0] = 63; x[:, 6, :, W - 1] = 63; dl[:, 6, :, 0] = -63; dl[:, 6, :, L - 1] = -63
    return pack(x, su, co, dl, la, lb, wt, th)
def setup_inputs_corners(rng):
    x, su, co, dl, la, lb, wt, th = parts(rng); th[:] = 0; dl = 126 * rng.integers(0, 2, (N, 8, 16, L)) - 63
    for r in range(N):
        own = spots(dl[r], wt[r]); come = spots(dl[r - 1], wt[r])
        for i in range(8):
            p = np.unique(own[i]); z = p[:0]
            if i % 2: z = p; p = np.setdiff1d(come[i], z)
            n = int(rng.choice(np.array([0, 1, CAP - 1, CAP, CAP + 1, W - H])))
            if r in (0, N - 1): n = (CAP, CAP, CAP + 1, CAP + 1, CAP - 1, CAP - 1, 0, 1)[i]
            if r == 1 and i in (2, 6): n = W - H
            n = min(n, 16 * len(p), W - H)
            a = np.concatenate([z, p]); s = np.stack([rng.permutation(H)[:len(a)] for k in range(16)])
            c = s[:, len(z):].copy().reshape(-1); c[rng.permutation(len(c))[:n]] = H + rng.permutation(W - H)[:n]
            s[:, len(z):] = c.reshape(16, -1)
            rest = np.ones(W, bool); rest[a] = False
            for k in range(16):
                free = np.ones(W, bool); free[s[k]] = False
                co[r, i, k, a] = s[k]; co[r, i, k, rest] = rng.permutation(np.flatnonzero(free))
    return pack(x, su, co, dl, la, lb, wt, th)
def setup_inputs_crowd(rng):
    x, su, co, dl, la, lb, wt, th = parts(rng)
    dl[:, :2] = 126 * rng.integers(0, 2, (N, 2, 16, L)) - 63
    for i in range(8):
        m = (1, 1, 2, 1, 4, 1, 2, 1)[i]; s = rng.integers(0, m, L); z = int(rng.integers(1, L - 1))
        if i % 2: s[z] = m
        la[:, i] = la[:, i][:, s]; lb[:, i] = lb[:, i][:, s]; dl[:, i] = dl[:, i][:, :, s]
    for r in range(N):
        n = spots(dl[r], wt[r])
        put(co[r, 0], int(n[0, 0]), np.full(16, W - 1)); put(co[r, 1], int(n[1, 0]), np.full(16, H))
        if r % 3 < 2: th[r] = 0
        if r % 3 == 0: dl[r, 5, :, L - 1] = 0; lb[r, 5, L - 1] = la[r, 5, L - 1]
        if r % 3 == 1: th[r, 3] = 1; dl[r, 3, :, L - 1] = 0; lb[r, 3, L - 1] = la[r, 3, L - 1]
    return pack(x, su, co, dl, la, lb, wt, th)
def setup_inputs_ties(rng):
    x, su, co, dl, la, lb, wt, th = parts(rng)
    x = 8 * (x >> 4); x[:, 1::2] = 63 - x[:, 1::2]; dl = 8 * rng.integers(-1, 2, (N, 8, 16, L))
    x[:, 3] = 63; x[:, 3, :7] = 62 + np.minimum(rng.integers(0, 4, (N, 7, W)), 1); dl[:, 3] = -63; dl[2, 3, :, 48:] = 0
    put(co[2, 3], 0, H + np.arange(16)); su[2, 3, :, H:H + 16] = H + ((np.arange(16) + 1) & 15)
    su[:, ::2, :, :W // 2] = su[:, ::2, :1, :W // 2].copy()
    la[:, :, 16:32] = la[:, :, :16].copy(); lb[:, :, 16:32] = lb[:, :, :16].copy(); dl[:, :, :, 16:32] = dl[:, :, :, :16].copy()
    lb[:, :, 32:48] = la[:, :, 32:48].copy(); dl[:, :, :, 32:48] = 0
    for r in range(N):
        dd = np.sum(np.abs(at(x[r], pick(co[r], lb[r])) - moved(at(x[r], pick(co[r], la[r])), dl[r])), axis=1)
        th[r] = np.sort(np.min(dd, axis=1), axis=1)[:, L // 2]; th[r, 4:] += rng.integers(0, 2, 4)
        if r == 2: th[r] = 1023; th[r, 3] = np.min(dd[3, :, :32])
    return pack(x, su, co, dl, la, lb, wt, th)
def check_inputs(d):
    bad = []
    for k, lo, hi in (("x0", 0, 63), ("su", 0, W - 1), ("co", 0, W - 1), ("dl", -63, 63), ("la", 0, W - 1), ("lb", 0, W - 1), ("wt", 0, 255), ("th", 0, 1023)):
        a = np.asarray(d[k]).astype(np.float64)
        if not (np.min(a) >= lo and np.max(a) <= hi): bad.append("range of " + k)
        if np.any(a != np.floor(a)): bad.append("whole numbers of " + k)
    if np.any(np.sort(np.asarray(d["co"]), axis=-1) != np.arange(W)): bad.append("a row of co holds every node once")
    return bad
def reference(x0, su, co, dl, la, lb, wt, th):
    x = x0.astype(np.float32).astype(np.int32).reshape(N, 8, 16, W); s = su.astype(np.int64).reshape(N, 8, 16, W); c = co.astype(np.int64).reshape(N, 8, 16, W)
    sh = dl.astype(np.float32).astype(np.int32).reshape(N, 8, 16, L); w = wt.astype(np.float32).astype(np.int32).reshape(N, 8, 16, 1, 1); lim = th.astype(np.int64).reshape(N, 8, 1)
    a = np.stack([gentries(v) for v in la]).astype(np.int64); b = np.stack([gentries(v) for v in lb]).astype(np.int64)
    flag = np.zeros((N, 8, W), bool); last = np.zeros(N, np.int64)
    for t in range(RO):
        for r in range(N):
            q = (r - t) % N
            d = pick(c[r], a[q]); f = pick(c[r], b[q])
            dist = np.sum(np.abs(at(x[r], f) - moved(at(x[r], d), sh[q])), axis=1)
            k = np.argmin(dist, axis=1)[:, None, :]
            dk = np.take_along_axis(d, k, 1)[:, 0]; fk = np.take_along_axis(f, k, 1)[:, 0]
            same = np.take_along_axis(dist, k, 1)[:, 0] < lim[r] + (last[r] & 63)
            e = moved(at(x[r], pick(s[r], dk)), sh[q])
            n = spot(np.sum(w[r] * e, axis=1).astype(np.int64) & 4095)
            j = np.argmax(np.sum(np.abs(at(x[r], n) - e), axis=1), axis=1)[:, None, :]
            nj = np.take_along_axis(n, j, 1)[:, 0]; ej = np.take_along_axis(e, j[:, None], 2)[:, :, 0]
            for i in range(8):
                lane = np.flatnonzero(~same[i]); place, first = np.unique(nj[i, lane], return_index=True)
                x[r, i][:, place] = ej[i][:, lane[first]]
                flag[r, i, c[r, i][:, place].reshape(-1)] = True; flag[r, i, :H] = False
                v = np.flatnonzero(flag[r, i])[:CAP]
                z = x[r, i][:, s[r, i][:, v]]
                x[r, i][:, v] = (np.max(z, axis=1) + np.min(z, axis=1)) >> 1
                flag[r, i, v] = False
            last[r] = np.sum(~same)
            a[q] = np.where(same, dk, a[q]); b[q] = np.where(same, fk, b[q])
    return {"yx": x.reshape(N, 128, W).astype(np.float32).astype(BF), "ya": np.stack([gtable(a[(r - RO + 1) % N]) for r in range(N)]).astype(np.float32),
            "yb": np.stack([gtable(b[(r - RO + 1) % N]) for r in range(N)]).astype(np.float32)}

from concourse.mybir import dt, AluOpType, AxisListType, ActivationFunctionType
A = AluOpType
F = ActivationFunctionType
B2, F4, I4, U2, H2 = "bfloat16", "float32", "int32", "uint16", "float16"
SB = lambda w, d: ("sbuf", [128] + w, d)
CH = [(0, 8), (8, 8)]
NC = len(CH)
QM = max(q for _, q in CH)
VFUSED = ((1, 1, 0), (1, 1, 1), (2, 0, 0), (2, 1, 0))
VFLAG = (2, 8)
VREP = (6, 0, 4)
VREN = 1
SCRATCH = {}


def declare(d, **kw):
    for names, w in kw.items():
        for n in names.split("_"):
            SCRATCH[n] = SB(list(w), d)


declare(B2, xw=[1536], wtb=[1], dl0_dl1_dl2_rdl=[256], rep0_rep1_rep2=[4096], blk_rge_tri_trx_idb_idn_oneb_kc2_kc3=[128],
        lr_ww=[16, 128], rx_rn_fsb=[768], t0_t1_mb0_mb1_g0_g1=[1024], e=[4096], upb=[48], fv=[1536], gr_mx_mn=[3072])
declare(I4, coe_sue=[1536], lai=[32], thi_pi=[1], pr=[3], di_dm2=[32], ai=[2], ui_ua_ub_uc_un=[16 * QM], i2=[3 * QM], si=[192])
declare(U2, ab0_ab1_ab2_rab1_rab2_abo1_abo2=[32], df=[512], dlist_ne16_nw16_eo16=[16], c16=[16 * QM], pos=[48], vl=[12], sv=[192])
declare(F4, abf_abn_abd_df32_al=[32], pf=[4], opar_thf_thq_thr_asum_tha=[1], rowg_dif_e8_onef=[128], rowr_kc1_dT=[512], it=[1536],
        rmin_rmax=[32 * QM], q16_lcol_dump_ebase_ald_nef=[16], v48_dv_dv1_z48_up0_fl_r0_r1_r2_r3_r4=[48], dm_sm_cmm_cms_sm2=[192], kd_kk_kk2_zf=[32 * QM],
        sma=[3 * QM], smb=[QM], fs0_fs1=[1536], cmp=[960])
declare(H2, m00_m01_m10_m11=[128], dfh_ta=[16, 2, 16], nh_na=[QM // 2, 2, 16], nr=[16 * QM])
for _c, (_q0, _q) in enumerate(CH):
    SCRATCH["a%d" % _c] = SB([_q, 16, 16], B2)
    for _n in ("s16%d", "n16%d"):
        SCRATCH[_n % _c] = SB([16 * _q], U2)
    SCRATCH["ct%d" % _c] = SB([16, _q], U2)
    SCRATCH["ew%d" % _c] = SB([16 * _q], B2)
    SCRATCH["eq%d" % _c] = SB([_q * (16 * _q + 2)], B2)
    SCRATCH["cwi%d" % _q] = SB([_q * (16 * _q + 2)], F4)
    SCRATCH["cw%d" % _q] = SB([_q * (16 * _q + 2)], B2)
SCRATCH["we"] = SB([QM * (16 * QM + 2)], B2)
for _n in ("py0", "py1"):
    SCRATCH[_n] = ("psum", [128, 32, 2, 16], F4)
for _n in ("kp0", "kp1", "ps0", "ps1"):
    SCRATCH[_n] = ("psum", [128, 512], F4)

PACK = {}


def pack(buf, d, names):
    n = 0
    for x in names.split():
        w = SCRATCH.pop(x)[1][1]
        PACK[x] = (buf, n, w)
        n += w + w % 2
    SCRATCH[buf] = SB([n], d)


pack("pkf", F4, "pf opar thf thq thr asum tha q16 lcol dump ebase ald nef v48 dv dv1 z48 up0 fl r0 r1 r2 r3 r4 sma smb abf abd df32 al")
pack("pki", I4, "pi pr di dm2 ai i2")
pack("pku", U2, "dlist ne16 nw16 eo16 pos vl")
SEMAPHORES = ["cv", "cs", "ct", "cg", "ls", "rdl", "rab1", "rab2", "adl1", "adl2", "aab1", "aab2", "ox"] + ["ld%d" % n for n in range(16)] + ["o%d" % n for n in range(8)]
SIZE = {B2: 2, F4: 4, I4: 4, U2: 2, H2: 2}
INFO = {}


def relay_of(src, dst, topo):
    if topo.may_write(src, dst):
        return None
    c = [x for x in topo.cores_of(src) if x != src and topo.may_write(x, dst)]
    c.sort(key=lambda x: (topo.die(x) != topo.die(src), x))
    return c[0]


def send(g, T, topo, src, dst, out, in_, rsem):
    rid, pid = topo.addr(dst, src)
    g.remote_dma(out, in_, T.sem[rsem], T.sem.ls, pid, rid, topo.mask(src, dst))
    return len(topo.engines(src, dst))


def relay_program(g, core, T, topo, src):
    i = T.rank_of(src)
    d1, d2 = T.cores[(i + 1) % 8], T.cores[(i + 2) % 8]
    n1 = relay_of(src, d1, topo) == core
    n2 = relay_of(src, d2, topo) == core
    k = len(topo.engines(src, core))
    n = 0
    g.wait_ge(T.sem.rdl, k)
    if n1:
        n += send(g, T, topo, core, d1, T.dl1[:], T.rdl[:], "adl1")
    if n2:
        n += send(g, T, topo, core, d2, T.dl2[:], T.rdl[:], "adl2")
    if n1:
        for t in (1, 2):
            g.wait_ge(T.sem["rab%d" % t], k)
            n += send(g, T, topo, core, d1, T["ab%d" % t][:], T["rab%d" % t][:], "aab%d" % t)
    g.wait_ge(T.sem.ls, n)


def s_(a, b, c=None):
    return slice(a, b, c)


def rank_program(g, core, T, topo):
    rank = T.rank_of(core)
    if rank is None:
        for src in T.cores:
            if core in topo.cores_of(src):
                i = T.rank_of(src)
                if core in [relay_of(src, T.cores[(i + s) % 8], topo) for s in (1, 2)]:
                    relay_program(g, core, T, topo, src)
        return
    ops = []
    acc = {}

    def ap(name, *ix, p=None):
        if name in PACK:
            name, o, w = PACK[name]
            r = range(*(ix[0] if ix else slice(None)).indices(w))
            ix = (slice(o + r[0], o + r[-1] + 1, r.step),)
        sh = SCRATCH[name][1][1:]
        ix = list(ix) + [slice(None)] * (len(sh) - len(ix))
        st, lo, hi, n = 1, 0, 0, 1
        for d in range(len(sh) - 1, -1, -1):
            x = ix[d]
            if isinstance(x, slice):
                r = range(*x.indices(sh[d]))
                lo, hi, n = lo + r[0] * st, hi + r[-1] * st, n * len(r)
            else:
                lo, hi = lo + x * st, hi + x * st
            st *= sh[d]
        ps = SCRATCH[name][0] == "psum"
        if ps:
            lo, hi = 0, st
        return {"ap": T[name][tuple([slice(None) if p is None else slice(0, p)] + ix)], "k": [(name, lo, hi + 1)], "n": n,
                "b": SIZE[SCRATCH[name][2]], "ps": ps, "ind": False}

    def ind(w, o):
        r = dict(w)
        r.update({"ap": w["ap"].indirect(o["ap"]), "k": w["k"] + o["k"], "n": 16 * o["n"], "ind": True})
        return r

    def op(eng, cost, outs, ins, fn, sem=None, val=1, lat=0.0):
        i = len(ops)
        wait, order = set(), set()
        rk = [k for o in ins for k in o["k"]] + [k for o in outs for k in o["k"][1:]]
        wk = [o["k"][0] for o in outs]
        for kind, keys in (("r", rk), ("w", wk)):
            for name, lo, hi in keys:
                psum = SCRATCH[name][0] == "psum"
                for (l2, h2, j, k2) in acc.get(name, []):
                    if j == i or l2 >= hi or h2 <= lo:
                        continue
                    if kind == "r" and k2 == "r" and not (psum and ops[j]["eng"] != eng):
                        continue
                    if psum and eng == "T" and ops[j]["eng"] == "T":
                        order.add(j)
                    else:
                        wait.add(j)
        for kind, keys in (("r", rk), ("w", wk)):
            for name, lo, hi in keys:
                lst = acc.setdefault(name, [])
                if kind == "w":
                    lst[:] = [x for x in lst if not (lo <= x[0] and x[1] <= hi)]
                lst.append((lo, hi, i, kind))
        ops.append({"eng": eng, "cost": cost, "fn": fn, "wait": wait, "order": order - wait, "sem": sem, "val": val, "lat": lat})
        return i

    def vcost(o, ins, tt=False):
        for x in [o] + ins:
            if x["ind"]:
                return 60 + x["n"] * (3.8 if x is o else 1.56)
        if tt:
            return 60 + max(64, o["n"] * (1 if any(x["ps"] for x in ins) else 2))
        return 60 + max(64, o["n"] * (0.5 if all(x["b"] == 2 for x in [o] + ins) else 1))

    def cp(o, i):
        op("V", vcost(o, [i]), [o], [i], lambda q: q.tensor_copy(o["ap"], i["ap"]))

    def tt(o, a, b, f):
        op("V", vcost(o, [a, b], True), [o], [a, b], lambda q: q.tensor_tensor(o["ap"], a["ap"], b["ap"], f))

    def ts(o, a, s1, f1, s2=None, f2=None):
        sc = [x for x in (s1, s2) if isinstance(x, dict)]
        v = [x["ap"] if isinstance(x, dict) else x for x in (s1, s2)]
        if f2 is None:
            op("V", vcost(o, [a]), [o], [a] + sc, lambda q: q.tensor_scalar(o["ap"], a["ap"], v[0], None, f1))
        else:
            op("V", vcost(o, [a]), [o], [a] + sc, lambda q: q.tensor_scalar(o["ap"], a["ap"], v[0], v[1], f1, f2))

    def scan(o, a, b, init, f1, f2):
        op("V", vcost(o, [a, b]), [o], [a, b], lambda q: q.tensor_tensor_scan(o["ap"], a["ap"], b["ap"], init, f1, f2))

    def trans(o, i):
        op("V", vcost(o, [i]), [o], [i], lambda q: q.transpose(o["ap"], i["ap"]))

    def fill(o, c):
        op("V", vcost(o, []), [o], [], lambda q: q.memset(o["ap"], c))

    def act(o, i, f, scale=None):
        n = i["n"] if i["ind"] else o["n"] if o["ind"] else i["n"]
        cost = 80 + (n * 1.56 if i["ind"] else n * 3.8 if o["ind"] else max(64, n))
        if scale is None:
            op("S", cost, [o], [i], lambda q: q.activation(o["ap"], i["ap"], f))
        else:
            op("S", cost, [o], [i], lambda q: q.activation(o["ap"], i["ap"], f, 0.0, scale))

    def mms(lst):
        cost = 60 + sum(max(64, x[2]["n"]) * (4 if x[2]["b"] == 4 else 1) for x in lst)

        def fn(q):
            for o, l, r, a, z in lst:
                m = q.matmul(o["ap"], l["ap"], r["ap"], a, z)
            return m
        op("T", cost, [x[0] for x in lst], [y for x in lst for y in x[1:3]], fn)

    def load(eng, buf, src, n):
        q = {"Y": g.sync, "S": g.scalar}[eng]
        op(eng, 100, [buf], [], lambda _q: q.dma_start(buf["ap"], src), sem="ld%d" % n, val=16, lat=2500)

    def store(dst, buf, sem):
        op("Y", 100, [], [buf], lambda _q: g.sync.dma_start(dst, buf["ap"]), sem=sem, val=16, lat=2500)

    def iota(o, pat, base, mult):
        if o["k"][0][0] in ("coe", "pki", "sue"):
            op("G", 130 + 2 * o["n"], [o], [], lambda q: q.iota(o["ap"], pat, base, mult))
        else:
            op("G", 130 + 2 * o["n"], [o], [], lambda q: q.iota(o["ap"], pat, base, mult, allow_small_or_imprecise_dtypes=True))

    loc = [0]

    def remote(stage, hops):
        for dst, land, rsem in hops:
            def fn(q, dst=dst, land=land, rsem=rsem):
                loc[0] += send(g, T, topo, core, dst, T[land][:], stage["ap"], rsem)
            i = op("G", 500, [], [stage], fn, sem="ls", val=0)
        return i

    def arrive(land, rsem, src, after, lat):
        rl = relay_of(src, core, topo)
        n = len(topo.engines(src if rl is None else rl, core))
        i = op("N", 0, [ap(land)], [], lambda q: None, sem=rsem, val=n, lat=lat)
        ops[i]["wait"].add(after)

    nxt, nx2, prv, pr2 = [T.cores[(rank + s) % 8] for s in (1, 2, -1, -2)]
    r1, r2 = relay_of(core, nxt, topo), relay_of(core, nx2, topo)
    a_ = s_(None, None)
    rcol = lambda: ap("pf", s_(0, 1))
    flipm = [["m00", "m01"], ["m10", "m11"]]

    def inputs():
        n = 0
        for c, (q0, q) in enumerate(CH):
            load("Y", ap("lai", s_(2 * q0, 2 * q0 + q)), T.la[:, q0:q0 + q], n)
            load("S", ap("lai", s_(2 * q0 + q, 2 * q0 + 2 * q)), T.lb[:, q0:q0 + q], n + 1)
            n += 2
        load("Y", ap("coe", s_(0, 1280)), T.co[:], n)
        load("S", ap("dl0"), T.dl[:], n + 1)
        load("Y", ap("xw", s_(0, 1280)), T.x0[:], n + 2)
        load("S", ap("thi", p=8), T.th[:], n + 3)
        load("S", ap("wtb"), T.wt[:], n + 4)
        load("Y", ap("sue", s_(0, 1280)), T.su[:], n + 5)

    def consts_a():
        iota(ap("pi"), [[0, 1]], 0, 1)
        iota(ap("dif"), [[1, 128]], 0, -1)
        iota(ap("rowg"), [[1, 8], [0, 16]], 0, 0)
        iota(ap("rowr"), [[0, 32], [1, 16]], 0, 0)
        ts(ap("pr", s_(0, 1)), ap("pi"), 15, A.bitwise_and)
        ts(ap("pr", s_(1, 2)), ap("pi"), 4, A.arith_shift_right)
        ts(ap("pr", s_(2, 3)), ap("pi"), 4, A.arith_shift_right, 1, A.bitwise_and)
        cp(ap("pf", s_(0, 3)), ap("pr"))
        cp(ap("pf", s_(3, 4)), ap("pi"))
        par = ap("pf", s_(2, 3))
        ts(ap("opar"), par, -1.0, A.mult, 1.0, A.add)
        ts(ap("idb"), ap("dif"), 0.0, A.is_equal)
        ts(ap("idn"), ap("dif"), 0.0, A.is_equal, -1.0, A.mult)
        ts(ap("m00"), ap("dif"), 0.0, A.is_equal, ap("opar"), A.mult)
        ts(ap("m11"), ap("dif"), 0.0, A.is_equal, par, A.mult)
        ts(ap("m01"), ap("dif"), 16.0, A.is_equal, ap("opar"), A.mult)
        ts(ap("m10"), ap("dif"), -16.0, A.is_equal, par, A.mult)
        ts(ap("blk"), ap("rowg"), ap("pf", s_(1, 2)), A.is_equal)
        ts(ap("kc1"), ap("rowr"), 2048.0, A.mult, -16777216.0, A.add)
        fill(ap("lr"), 0.0)
        for r in range(16):
            act(ap("lr", r, s_(r, 128, 16)), ap("blk", s_(r, 128, 16)), F.Copy, 32768.0)

    def consts_b():
        w = 32 * QM
        ts(ap("rmin"), ap("rowr", s_(0, w)), 0.0, A.is_equal, 268435456.0, A.mult)
        ts(ap("rmin"), ap("rmin"), -134217728.0, A.add)
        ts(ap("rmax"), ap("rmin"), -1.0, A.mult)
        ts(ap("kc2"), ap("rowr", s_(0, 128)), -512.0, A.mult, 7680.0, A.add)
        fill(ap("kc3"), -16777216.0)
        cp(ap("thf", p=8), ap("thi", p=8))
        ts(ap("e8", p=8), ap("rowg", p=8), ap("pf", s_(3, 4), p=8), A.is_equal)
        mms([(ap("ps0", s_(0, 1)), ap("e8", p=8), ap("thf", p=8), True, True)])
        cp(ap("thq"), ap("ps0", s_(0, 1)))
        ts(ap("thr"), ap("thq"), 32768.0, A.mult, -16777216.0, A.add)
        fill(ap("ww"), 0.0)
        for j in range(16):
            ts(ap("ww", j, s_(j, 128, 16)), ap("blk", s_(j, 128, 16)), ap("wtb"), A.mult)
        iota(ap("q16"), [[16, 16]], 0, 0)
        ts(ap("lcol"), ap("q16"), rcol(), A.add)
        ts(ap("dump"), ap("lcol"), 1280.0, A.add)
        iota(ap("it"), [[1, 1536]], 0, 0)
        for c, (q0, q) in enumerate(CH):
            iota(ap("eq%d" % c), [[0, q * (16 * q + 2)]], 0, 0)
            ts(ap("ebase", s_(q0, q0 + q)), ap("lcol", s_(0, q)), 16.0, A.mult, 15.0, A.add)
        iota(ap("coe", s_(1280, 1536)), [[1, 256]], 1280, 0)
        for q in sorted({q for _, q in CH}):
            w, n = 16 * q + 2, q * (16 * q + 2)
            iota(ap("cwi%d" % q), [[-16, q], [1, w]], -2, 0)
            ts(ap("cwi%d" % q), ap("cwi%d" % q), rcol(), A.is_equal, 1023.0, A.mult)
            ts(ap("cw%d" % q), ap("cwi%d" % q), 1.0, A.add)
            fill(ap("cw%d" % q, s_(0, n, w)), 0.0)
            fill(ap("cw%d" % q, s_(1, n, w)), 0.0)

    def consts_c():
        fill(ap("oneb"), 1.0)
        fill(ap("onef"), 1.0)
        fill(ap("zf"), 0.0)
        fill(ap("z48"), 0.0)
        fill(ap("fl"), 0.0)
        iota(ap("xw", s_(1280, 1536)), [[0, 256]], 0, 0)
        iota(ap("sue", s_(1280, 1536)), [[0, 256]], 0, 0)
        iota(ap("v48"), [[16, 48]], 192, 0)
        ts(ap("rge"), ap("rowr", s_(0, 128)), rcol(), A.is_ge)
        tt(ap("tri"), ap("rge"), ap("blk"), A.mult)
        tt(ap("trx"), ap("tri"), ap("blk"), A.subtract)
        ts(ap("dv"), ap("v48"), rcol(), A.add)
        ts(ap("dv1"), ap("dv"), 1.0, A.add)
        ts(ap("dm"), ap("rowr", s_(0, 192)), rcol(), A.is_equal)
        ts(ap("sm"), ap("rowr", s_(0, 192)), 0.0, A.is_gt)
        for h in range(2):
            ts(ap("rx", s_(384 * h, 384 * h + 384)), ap("rowr", s_(0, 384)), 0.0, A.is_gt)
            ts(ap("rn", s_(384 * h, 384 * h + 384)), ap("rowr", s_(0, 384)), 0.0, A.is_equal, 64.0, A.mult)

    def reps(t):
        for k in range(16):
            if k < VREP[t]:
                cp(ap("rep%d" % t, s_(k, 4096, 16)), ap("dl%d" % t))
            else:
                act(ap("rep%d" % t, s_(k, 4096, 16)), ap("dl%d" % t), F.Copy)

    def rnd(t):
        rep, ab, last = "rep%d" % t, "ab%d" % t, t == 2
        xall, base = ap("xw", s_(0, 1280)), ap("xw", s_(0, 512))
        if t == 0:
            cp(ap("ab0"), ap("lai"))
        cp(ap("df"), ind(ap("coe", s_(0, 1280)), ap(ab)))
        cp(ap("abf"), ap(ab))
        cp(ap("dfh"), ap("df"))
        trans(ap("ta"), ap("dfh"))
        mms([(ap("py1", s_(0, 16), c1), ap(flipm[c1][gp]), ap("ta", a_, gp), gp == 0, gp == 1) for c1 in (0, 1) for gp in (0, 1)])
        tt(ap("dT"), ap("py1", s_(0, 16)), ap("kc1"), A.add)
        fs, fv = "fs%d" % (t % 2), "fv"
        iota(ap(fs, s_(512, 1280)), [[0, 768]], 0, 0)
        iota(ap(fv, s_(512, 1280)), [[0, 768]], 0, 0)

        def second(c, h, w, off, m, fused):
            dst = ap("a%d" % c, s_(4 * h, 4 * h + 4))
            z = h % 2
            if fused:
                tt(ap("g%d" % z), ind(w, off), m, A.subtract)
                act(dst, ap("g%d" % z), F.Abs)
            else:
                act(ap("g%d" % z), ind(w, off), F.Identity)
                nm, lo = m["k"][0][0], m["k"][0][1]
                mms([(ap("py%d" % z, s_(16 * i, 16 * i + 16)), ap("idb"), ap("g%d" % z, s_(512 * i, 512 * i + 512)), True, False) for i in (0, 1)] +
                    [(ap("py%d" % z, s_(16 * i, 16 * i + 16)), ap("idn"), ap(nm, s_(lo + 512 * i, lo + 512 * i + 512)), False, True) for i in (0, 1)])
                act(dst, ap("py%d" % z), F.Abs)

        def sums(c, h, first, stop):
            o = ap("kp%d" % (c % 2), s_(64 * h, 64 * h + 64))
            mms([(o, ap("lr", r), ap("a%d" % c, s_(4 * h, 4 * h + 4), r), first and r == 0, stop and r == 15) for r in range(16)])

        def step1(c):
            q0, q = CH[c]
            w = 16 * q
            for h in range(q // 4):
                z = h % 2
                lo, o = 256 * q0 + 1024 * h, 32 * q0 + 64 * h
                tt(ap("t%d" % z), ind(xall, ap("df", s_(o, o + 64))), ap(rep, s_(lo, lo + 1024)), A.add)
                ts(ap("mb%d" % z), ap("t%d" % z), 0.0, A.max, 63.0, A.min)
                second(c, h, xall, ap("df", s_(o + w, o + w + 64)), ap("mb%d" % z), (1, c, h) in VFUSED)
                sums(c, h, True, True)
            kq = ap("kp%d" % (c % 2), s_(0, w))
            for i in (0, 1):
                tt(ap("kd", s_(w * i, w * i + w)), kq, ap("dT", s_(32 * q0 + w * i, 32 * q0 + w * i + w)), A.add)
            scan(ap("kk", s_(0, 2 * w)), ap("rmin", s_(0, 2 * w)), ap("kd", s_(0, 2 * w)), 134217728.0, A.max, A.min)
            both, first = s_(2 * q0, 2 * q0 + 2 * q), s_(2 * q0, 2 * q0 + q)
            cp(ap("di", both), ap("kk", s_(15, 2 * w, 16)))
            ts(ap("dm2", both), ap("di", both), 2047, A.bitwise_and)
            cp(ap("dlist", s_(q0, q0 + q)), ap("dm2", first))
            ts(ap("al", both), ap("kk", s_(15, 2 * w, 16)), ap("thr"), A.is_lt)
            tt(ap("ald", s_(q0, q0 + q)), ap("al", first), ap("dump", s_(q0, q0 + q)), A.mult)

        def lanes():
            cp(ap("df32"), ap("dm2"))
            tt(ap("abd"), ap("df32"), ap("abf"), A.subtract)
            tt(ap("abd"), ap("abd"), ap("al"), A.mult)
            tt(ap("abn"), ap("abf"), ap("abd"), A.add)
            if last:
                for c, (q0, q) in enumerate(CH):
                    store(T.ya[:, q0:q0 + q], ap("abn", s_(2 * q0, 2 * q0 + q)), "o%d" % (2 * c))
                    store(T.yb[:, q0:q0 + q], ap("abn", s_(2 * q0 + q, 2 * q0 + 2 * q)), "o%d" % (2 * c + 1))
                return
            k = t + 1
            cp(ap("abo%d" % k), ap("abn"))
            i = remote(ap("abo%d" % k), [(nxt, "ab%d" % k, "aab%d" % k) if r1 is None else (r1, "rab%d" % k, "rab%d" % k)])
            arrive("ab%d" % k, "aab%d" % k, prv, i, 8000)

        def threshold():
            asum, al = ap("asum"), ap("al")
            op("V", 124, [asum], [al], lambda q: q.tensor_reduce(asum["ap"], al["ap"], AxisListType.X, A.add))
            mms([(ap("ps1", s_(0, 1)), ap("onef"), ap("asum"), True, True)])
            ts(ap("ai", s_(0, 1)), ap("ps1", s_(0, 1)), -0.5, A.mult, 2048.0, A.add)
            ts(ap("ai", s_(1, 2)), ap("ai", s_(0, 1)), 63, A.bitwise_and)
            tt(ap("tha"), ap("thq"), ap("ai", s_(1, 2)), A.add)
            ts(ap("thr"), ap("tha"), 32768.0, A.mult, -16777216.0, A.add)

        def step2a(c):
            q0, q = CH[c]
            w = 16 * q
            x = s_(0, w)
            s16, n16 = "s16%d" % c, "n16%d" % c
            u = ap("ps%d" % (c % 2), x)
            cp(ap(s16), ind(ap("sue", s_(0, 1280)), ap("dlist", s_(q0, q0 + q))))
            for h in range(q // 4):
                z, lo = h % 2, 256 * q0 + 1024 * h
                tt(ap("t%d" % z), ind(xall, ap(s16, s_(64 * h, 64 * h + 64))), ap(rep, s_(lo, lo + 1024)), A.add)
                ts(ap("e", s_(lo, lo + 1024)), ap("t%d" % z), 0.0, A.max, 63.0, A.min)
                mms([(ap("ps%d" % (c % 2), s_(64 * h, 64 * h + 64)), ap("ww", j), ap("e", s_(lo + j, lo + 1024, 16)), j == 0, j == 15) for j in range(16)])
            cp(ap("ui", x), u)
            ts(ap("ua", x), ap("ui", x), 4095, A.bitwise_and)
            ts(ap("ub", x), ap("ua", x), 1184.0, A.add)
            tt(ap("uc", x), ap("ua", x), ap("ub", x), A.mult)
            ts(ap("un", x), ap("uc", x), 5, A.arith_shift_right, 511, A.bitwise_and)
            cp(ap(n16), ap("un", x))
            b = s_(0, q // 2)
            cp(ap("nh", b), ap(n16))
            trans(ap("na", b), ap("nh", b))
            kp = "kp%d" % (c % 2)
            lst = [(ap(kp, x), ap("idb"), ap("kc3", x), True, False), (ap(kp, x), ap("idb"), ap("kc2", x), False, False)]
            for k in range(q):
                lst += [(ap(kp, s_(16 * k, 16 * k + 16)), ap(flipm[k % 2][gp]), ap("na", k // 2, gp), False, False) for gp in (0, 1)]
            mms(lst)

        def step2b(c):
            q0, q = CH[c]
            w = 16 * q
            n16 = "n16%d" % c
            for h in range(q // 4):
                lo = 256 * q0 + 1024 * h
                second(c, h, base, ap(n16, s_(64 * h, 64 * h + 64)), ap("e", s_(lo, lo + 1024)), (2, c, h) in VFUSED)
                sums(c, h, False, h == q // 4 - 1)
            kq = ap("kp%d" % (c % 2), s_(0, w))
            scan(ap("kk2", s_(0, w)), ap("rmax", s_(0, w)), kq, -134217728.0, A.min, A.max)
            q8 = s_(q0, q0 + q)
            i0, i1, i2 = s_(0, q), s_(QM, QM + q), s_(2 * QM, 2 * QM + q)
            cp(ap("i2", i0), ap("kk2", s_(15, w, 16)))
            ts(ap("i2", i1), ap("i2", i0), 511, A.bitwise_and)
            ts(ap("i2", i2), ap("i2", i0), 9, A.arith_shift_right, 15, A.bitwise_and)
            tt(ap("nef", q8), ap("i2", i1), ap("ald", q8), A.max)
            cp(ap("ne16", q8), ap("nef", q8))
            tt(ap("sma", i0), ap("ebase", q8), ap("i2", i2), A.subtract)
            cp(ap("eo16", q8), ap("sma", i0))
            cp(ap("nr", s_(0, w)), ind(ap("it"), ap("ne16", q8)))
            eq, v = "eq%d" % c, w + 2
            for k in range(q):
                ts(ap(eq, s_(v * k + 2, v * k + v)), ap("nr", s_(0, w)), ap("nef", s_(q0 + k, q0 + k + 1)), A.is_equal)
            scan(ap("we", s_(0, q * v)), ap(eq), ap("cw%d" % q), 0.0, A.add, A.mult)
            ts(ap("sma", i1), ap("we", s_(v - 1, q * v, v)), 1536.0, A.is_gt)
            tt(ap("sma", i2), ap("sma", i1), ap("dump", q8), A.mult)
            tt(ap("smb", i0), ap("sma", i2), ap("nef", q8), A.max)
            cp(ap("nw16", q8), ap("smb", i0))
            cp(ap("ew%d" % c), ind(ap("e", s_(256 * q0, 256 * (q0 + q))), ap("eo16", q8)))
            b = s_(0, q // 2)
            cp(ap("c16", s_(0, w)), ind(ap("coe"), ap("nw16", q8)))
            cp(ap("nh", b), ap("c16", s_(0, w)))
            trans(ap("na", b), ap("nh", b))
            pz = "ps%d" % (c % 2)
            mms([(ap(pz, s_(k, w, q)), ap(flipm[k % 2][gp]), ap("na", k // 2, gp), gp == 0, gp == 1) for k in range(q) for gp in (0, 1)])
            cp(ap("ct%d" % c), ap(pz, s_(0, w)))
            for k in range(16):
                if k < VFLAG[c]:
                    cp(ind(ap(fv), ap("ct%d" % c, k)), ap("oneb", s_(0, w)))
                else:
                    act(ind(ap(fs), ap("ct%d" % c, k)), ap("zf", s_(0, w)), F.Sigmoid)

        def step4():
            for c in range(NC - 1, -1, -1):
                q0, q = CH[c]
                cp(ind(ap("xw"), ap("nw16", s_(q0, q0 + q))), ap("ew%d" % c))
            act(ap("fsb"), ap(fs, s_(512, 1280)), F.Copy)
            o48 = ap("kp0", s_(0, 48))
            mms([(o48, ap("lr", r), ap(fv, s_(512 + r, 1280, 16)), r == 0, False) for r in range(16)])
            mms([(o48, ap("lr", r), ap("fsb", s_(r, 768, 16)), False, r == 15) for r in range(16)])
            ts(ap("up0"), o48, 0.0, A.is_gt)
            tt(ap("upb"), ap("up0"), ap("fl"), A.max)
            oa, ob = ap("kp0", s_(0, 48)), ap("kp0", s_(64, 112))
            mms([(oa, ap("blk"), ap("upb"), True, True), (ob, ap("trx"), ap("upb"), True, True)])
            scan(ap("r0"), oa, ap("z48"), 0.0, A.add, A.add)
            tt(ap("r1"), ap("r0"), ob, A.add)
            ts(ap("r2"), ap("r1"), 192.0, A.is_le)
            tt(ap("r3"), ap("r2"), ap("upb"), A.mult)
            tt(ap("r4"), ap("r1"), ap("dv1"), A.subtract)
            tt(ap("r4"), ap("r4"), ap("r3"), A.mult)
            tt(ap("r4"), ap("r4"), ap("dv"), A.add)
            cp(ap("pos"), ap("r4"))
            if not last:
                tt(ap("fl"), ap("upb"), ap("r3"), A.subtract)
            cp(ap("cmp", s_(0, 192)), ap("it", s_(1280, 1472)))
            cp(ind(ap("cmp"), ap("pos")), ap("it", s_(512, 1280)))
            tt(ap("cmm"), ap("cmp", s_(0, 192)), ap("dm"), A.mult)
            scan(ap("cms"), ap("sm"), ap("cmm"), 0.0, A.mult, A.max)
            cp(ap("vl"), ap("cms", s_(15, 192, 16)))
            cp(ap("sv"), ind(ap("sue"), ap("vl")))
            for i in range(4):
                x = s_(768 * i, 768 * i + 768)
                src = ind(xall, ap("sv", s_(48 * i, 48 * i + 48)))
                if i < VREN:
                    cp(ap("gr", x), src)
                else:
                    act(ap("gr", x), src, F.Identity)
                scan(ap("mx", x), ap("rx"), ap("gr", x), 0.0, A.mult, A.max)
                scan(ap("mn", x), ap("rn"), ap("gr", x), 0.0, A.max, A.min)
            tt(ap("sm2"), ap("mx", s_(15, 3072, 16)), ap("mn", s_(15, 3072, 16)), A.add)
            ts(ap("si"), ap("sm2"), 0.5, A.mult, -0.25, A.add)
            cp(ind(ap("xw"), ap("vl")), ap("si"))

        for c in range(NC):
            step1(c)
        step2a(0)
        lanes()
        if not last:
            threshold()
        for c in range(NC):
            if c:
                step2a(c)
            step2b(c)
        step4()
        if last:
            store(T.yx[:], xall, "ox")

    inputs()
    consts_a()
    reps(0)
    hops = []
    if r1 is None:
        hops.append((nxt, "dl1", "adl1"))
    if r2 is None:
        hops.append((nx2, "dl2", "adl2"))
    for r in sorted({x for x in (r1, r2) if x is not None}):
        hops.append((r, "rdl", "rdl"))
    snt = remote(ap("dl0"), hops)
    arrive("dl1", "adl1", prv, snt, 8000)
    arrive("dl2", "adl2", pr2, snt, 8000)
    consts_b()
    consts_c()
    rnd(0)
    reps(1)
    rnd(1)
    reps(2)
    rnd(2)

    n = len(ops)
    succ = [[] for _ in range(n)]
    npred = [0] * n
    for i, o in enumerate(ops):
        for j in o["wait"] | o["order"]:
            succ[j].append(i)
            npred[i] += 1
    prio = [0.0] * n
    for i in range(n - 1, -1, -1):
        o = ops[i]
        prio[i] = o["cost"] + o["lat"] + max([prio[j] for j in succ[i]], default=0.0)
    free = {}
    ready = {i: 0.0 for i in range(n) if npred[i] == 0}
    rt = [0.0] * n
    seq = []
    while ready:
        best = min(max(free.get(ops[i]["eng"], 0.0), r) for i, r in ready.items())
        cand = [i for i, r in ready.items() if max(free.get(ops[i]["eng"], 0.0), r) <= best + 1e-6]
        i = max(cand, key=lambda x: (prio[x], -x))
        del ready[i]
        o = ops[i]
        free[o["eng"]] = best + o["cost"] if o["eng"] != "N" else 0.0
        fin = best + o["cost"] + o["lat"]
        o["start"], o["fin"] = best, fin
        seq.append(i)
        for j in succ[i]:
            npred[j] -= 1
            k = fin + 40 if i in ops[j]["wait"] else best
            rt[j] = max(rt[j], k)
            if npred[j] == 0:
                ready[j] = rt[j]
    INFO["ops"] = ops

    queues = {"V": g.vector, "S": g.scalar, "T": g.tensor, "G": g, "Y": g.sync, "N": None}
    esem = {"V": "cv", "S": "cs", "T": "ct", "G": "cg"}
    count = {}
    known = {e: {} for e in queues}
    final = {}
    for i in seq:
        o = ops[i]
        e, q = o["eng"], queues[o["eng"]]
        if e != "N":
            for j in sorted(o["wait"], key=lambda x: -ops[x]["fin"]):
                s, v = ops[j]["done"]
                if v and known[e].get(s, 0) < v:
                    q.wait_ge(T.sem[s], v)
                    known[e][s] = v
                    for a, b in ops[j]["clk"].items():
                        known[e][a] = max(known[e].get(a, 0), b)
        ins = o["fn"](q)
        if o["sem"] is None:
            s = esem[e]
            count[s] = count.get(s, 0) + 1
            ins.then_inc(T.sem[s], 1)
            o["done"] = (s, count[s])
            final[s] = count[s]
        else:
            o["done"] = (o["sem"], o["val"])
            if o["val"]:
                if e != "N":
                    ins.then_inc(T.sem[o["sem"]], o["val"])
                final[o["sem"]] = o["val"]
        o["clk"] = dict(known[e]) if e != "N" else {}
    if loc[0]:
        final["ls"] = loc[0]
    for s in sorted(final):
        g.wait_ge(T.sem[s], final[s])
